import numpy as np
import ml_dtypes


def mxq(x, axis, fmt="e4m3"):
    dtype, down = {"e4m3": (ml_dtypes.float8_e4m3fn, 7), "e5m2": (ml_dtypes.float8_e5m2, 14)}[fmt]
    v = np.moveaxis(np.asarray(x, np.float32).astype(ml_dtypes.bfloat16).astype(np.float64), axis, -1)
    blocks = v.reshape(v.shape[:-1] + (-1, 32))
    amax = np.abs(blocks).max(-1, keepdims=True)
    byte = np.maximum(np.where(amax > 0, np.frexp(amax)[1] - 1 + 127, 0) - down, 1)
    scale = np.exp2(byte - 127.0)
    codes = (blocks / scale).astype(np.float32).astype(dtype).astype(np.float64)
    return np.moveaxis((codes * scale).reshape(v.shape), -1, axis)


WIDE = False


def mx_kscale(k):
    if not WIDE:
        return np.ones(k)
    levels = np.array([10, -10, 5, -5, 0])
    if k % 512:
        return np.exp2(np.random.permutation(np.resize(levels, k // 32))).repeat(32)
    a = np.empty((k // 512, 16))
    for p in range(k // 512):
        a[p, :8] = np.random.permutation(np.resize(levels, 8))
        for g in range(8):
            far = levels[np.abs(levels - a[p, g]) >= 10]
            a[p, g + 8] = far[np.random.randint(len(far))]
    return np.exp2(a.ravel()).repeat(32)


def f64(x):
    return np.asarray(x).astype(np.float64)


def striped(idx):
    return np.tile(np.asarray(idx).reshape(-1, 16).T, (8, 1)).astype(np.uint16)


def unstriped(offs):
    return offs[:16].T.reshape(-1).astype(np.int64)


E2M1 = np.array([0.0, 0.5, 1.0, 1.5, 2.0, 3.0, 4.0, 6.0, -0.0, -0.5, -1.0, -1.5, -2.0, -3.0, -4.0, -6.0])


def pack_weight(w, fmt):
    k, n = w.shape
    w = f64(np.asarray(w, np.float32).astype(ml_dtypes.bfloat16)).reshape(k // 32, 32, n)
    amax = np.abs(w).max(1)
    if fmt == "e4m3":
        byte = np.frexp(amax)[1] - 1 + 127 - 7
    else:
        mant, ex = np.frexp(amax / 6.0)
        byte = np.where(mant > 0.5, ex, ex - 1) + 127
    byte = np.clip(np.where(amax > 0, byte, 1), 1, 254)
    scaled = (w * np.exp2(127.0 - byte)[:, None, :]).reshape(k, n).astype(np.float32)
    by_word = np.ascontiguousarray(scaled.reshape(k // 512, 128, 4, n).transpose(0, 1, 3, 2))
    if fmt == "e4m3":
        words = by_word.astype(ml_dtypes.float8_e4m3fn).view(np.uint8)
    else:
        c = by_word.astype(ml_dtypes.float4_e2m1fn).view(np.uint8) & 0xF
        words = (c[..., 0::2] | (c[..., 1::2] << 4)).reshape(k // 512, 128, 2 * n)
    return np.ascontiguousarray(words), np.ascontiguousarray(byte.astype(np.uint8).reshape(k // 512, 16, n))


def unpack_weight(words, scales, fmt):
    g, _, n = scales.shape
    words = np.ascontiguousarray(words).reshape(g, 128, n, -1)
    if fmt == "e4m3":
        vals = words.view(ml_dtypes.float8_e4m3fn).astype(np.float64)
    else:
        nib = np.empty((g, 128, n, 4), np.uint8)
        nib[..., 0::2] = words & 0xF
        nib[..., 1::2] = words >> 4
        vals = E2M1[nib]
    vals = vals * np.repeat(np.exp2(scales.astype(np.float64) - 127.0), 8, axis=1)[..., None]
    return vals.transpose(0, 1, 3, 2).reshape(g * 512, n)


def sigmoid(v):
    return 1.0 / (1.0 + np.exp(-v))


K, R, F, T, J = 512, 128, 512, 2048, 512


def setup_inputs():
    n = np.random.standard_normal
    idx = np.random.permutation(T)[:J]
    idx2 = np.random.permutation(T)[:J]
    fk = mx_kscale(K)
    ff = mx_kscale(F)
    fj = mx_kscale(J)
    tj = np.ones(T)
    tj[idx2] = fj
    tabp = pack_weight(n((K, T)) / fk[:, None], "e2m1")
    tab2p = pack_weight(n((K, T)) / fk[:, None], "e2m1")
    return {
        "tab_words": tabp[0],
        "tab_scales": tabp[1],
        "w1": (n((K, R)) * 1 / np.sqrt(K) * fk[:, None]).astype(np.float32),
        "tab2_words": tab2p[0],
        "tab2_scales": tab2p[1],
        "w2": (n((K, R)) * 1 / np.sqrt(K) * fk[:, None]).astype(np.float32),
        "bias": (np.random.uniform(-0.5, 0.5, (R, 1))).astype(np.float32),
        "wo": (n((F, R)) * 1 / np.sqrt(F) * ff[:, None]).astype(np.float32),
        "dy": (n((F, J)) / ff[:, None]).astype(np.float32),
        "js": (np.random.uniform(0.5, 2.0, (1, J)) * fj).astype(np.float32),
        "xrows": (n((K, T)) / tj).astype(np.float32),
        "old": (n((K, R)) * 4.0).astype(np.float32),
        "offs": striped(idx),
        "offs2": striped(idx2),
    }


def reference(tab_words, tab_scales, w1, tab2_words, tab2_scales, w2, bias, wo, dy, js, xrows, old, offs, offs2):
    idx = unstriped(offs)
    idx2 = unstriped(offs2)
    tabu = unpack_weight(tab_words, tab_scales, "e2m1")
    tab2u = unpack_weight(tab2_words, tab2_scales, "e2m1")
    w1q = mxq(f64(w1), 0, "e4m3")
    tabidxg = tabu[:, idx]
    a = w1q.T @ tabidxg
    w2q = mxq(f64(w2), 0, "e4m3")
    tab2idx2g = tab2u[:, idx2]
    b = w2q.T @ tab2idx2g
    h1 = np.tanh(a)
    gt = sigmoid(b + f64(bias))
    woq = mxq(f64(wo), 0, "e4m3")
    dyq = mxq(f64(dy), 0, "e4m3")
    c0 = woq.T @ dyq
    dgt = c0 * h1
    db = dgt * gt * (1.0 - gt)
    gs = db * f64(js)
    gt1 = gs.T
    xt = f64(xrows)[:, idx2].T
    xtq = mxq(xt, 0, "e4m3")
    gt1q = mxq(gt1, 0, "e4m3")
    gw = xtq.T @ gt1q
    y = gw + f64(old)
    return y

@@ -1,0 +1,192 @@
+from contextlib import ExitStack
+
+import concourse.mybir as mybir
+from concourse.masks import make_identity
+
+K, R, F, T, J = 512, 128, 512, 2048, 512
+FLOPS = 2 * R * J * (K + K + F + K)
+
+F32 = mybir.dt.float32
+BF16 = mybir.dt.bfloat16
+I32 = mybir.dt.int32
+U32 = mybir.dt.uint32
+U16 = mybir.dt.uint16
+U8 = mybir.dt.uint8
+FP8X4 = mybir.dt.float8_e4m3fn_x4
+FP4X4 = mybir.dt.float4_e2m1fn_x4
+ACT = mybir.ActivationFunctionType
+ALU = mybir.AluOpType
+
+P = 128
+PACK = 4
+
+
+def tile_attend_ctwotables_b_w_kernel(
+    tc, tab_words, tab_scales, w1, tab2_words, tab2_scales, w2, bias, wo, dy, js, xrows, old, offs, offs2, out
+):
+    nc = tc.nc
+    with ExitStack() as ctx:
+        sb = ctx.enter_context(tc.tile_pool(name="sb", bufs=1))
+        ps = ctx.enter_context(tc.psum_pool(name="ps", bufs=1))
+        ps2 = ctx.enter_context(tc.psum_pool(name="ps2", bufs=2))
+
+        def tile(name, shape, dtype):
+            return sb.tile(shape, dtype, name=name, align_bytes=64)
+
+        def rows_by_four(src):
+            return src.rearrange("(p i) c -> p i c", i=PACK)
+
+        def load_words(name, words, lst):
+            word_win = tile(name + "_word_win", [P, T], U16)
+            nc.sync.dma_start(out=word_win[:].bitcast(I32), in_=words[0].bitcast(I32))
+            offsets = tile(name + "_offsets", [P, J // 16], U16)
+            nc.sync.dma_start(offsets[:], lst)
+            return word_win, offsets
+
+        def load_scales(name, scales):
+            scale_win = tile(name + "_scale_win", [P, T], U8)
+            nc.vector.memset(scale_win[:].bitcast(I32), 0)
+            for q in range(4):
+                nc.sync.dma_start(
+                    out=scale_win[32 * q : 32 * q + 4, :].bitcast(I32),
+                    in_=scales[0, 4 * q : 4 * q + 4, :].bitcast(I32),
+                )
+            return scale_win
+
+        def load(name, src, shape):
+            raw = tile(name, shape, F32)
+            nc.sync.dma_start(out=raw[:], in_=src)
+            return raw
+
+        bias_col = tile("bias_col", [P, 1], F32)
+        nc.gpsimd.dma_start(out=bias_col[:], in_=bias)
+        js_cols = tile("js_cols", [P, PACK], F32)
+        nc.gpsimd.dma_start(out=js_cols[:], in_=js.rearrange("o (p t) -> (o p) t", t=PACK))
+        ident = tile("ident", [P, P], F32)
+        make_identity(nc, ident[:])
+
+        word_win2, slots2 = load_words("t2", tab2_words, offs2)
+        scale_win2 = load_scales("t2", tab2_scales)
+        w2_raw = load("w2_raw", rows_by_four(w2), [P, PACK, R])
+        word_win1, slots1 = load_words("t1", tab_words, offs)
+        w1_raw = load("w1_raw", rows_by_four(w1), [P, PACK, R])
+        scale_win1 = load_scales("t1", tab_scales)
+        wo_raw = load("wo_raw", rows_by_four(wo), [P, PACK, R])
+        dy_raw = load("dy_raw", rows_by_four(dy), [P, PACK, J])
+        x_rows = rows_by_four(xrows)
+        x_win = [load("x_win%d" % c, x_rows[:, c, :], [P, T]) for c in range(PACK)]
+        old_sb = load("old_sb", rows_by_four(old), [P, PACK, R])
+
+        half_bias = tile("half_bias", [P, 1], F32)
+        nc.gpsimd.tensor_scalar(
+            out=half_bias[:], in0=bias_col[:], scalar1=0.5, scalar2=0.0, op0=ALU.mult, op1=ALU.add
+        )
+
+        def quantize(name, grouped, width, codes_tag=None):
+            codes = tile(codes_tag or name + "_codes", [P, width], U32)
+            scales = tile(name + "_scales", [P, width], U8)
+            nc.vector.quantize_mx(out=codes[:].bitcast(FP8X4), scales=scales[:], in_=grouped)
+            return codes, scales
+
+        def interleave(dst, raw):
+            nc.scalar.activation(
+                dst.rearrange("p (c n) i -> p c i n", n=4),
+                raw[:].rearrange("p i (c n) -> p c i n", n=4),
+                ACT.Copy,
+            )
+
+        def gather(name, window, offsets, dtype):
+            picked = tile(name, [P, J], dtype)
+            nc.vector.tensor_copy(picked[:], window[:].indirect(offsets[:]))
+            return picked
+
+        def weight(name, raw):
+            grouped = tile(name + "_grouped", [P, R, PACK], BF16)
+            interleave(grouped[:], raw)
+            return quantize(name, grouped[:].rearrange("p r i -> p (r i)"), R)
+
+        def layer(name, word_win, scale_win, slots, w_raw):
+            words = gather(name + "_words", word_win, slots, U16)
+            scales = gather(name + "_scale_bytes", scale_win, slots, U8)
+            w_codes, w_scales = weight(name + "_w", w_raw)
+            acc = ps.tile([P, J], F32, name=name + "_bank")
+            nc.tensor.matmul_mx(
+                out=acc[:], lhsT=w_codes[:].bitcast(FP8X4), lhsT_scale=w_scales[:],
+                rhs=words[:].bitcast(FP4X4), rhs_scale=scales[:], start=True, stop=True,
+            )
+            return acc[:].rearrange("r (s t) -> r t s", t=PACK)
+
+        b_dealt = layer("b", word_win2, scale_win2, slots2, w2_raw)
+        a_dealt = layer("a", word_win1, scale_win1, slots1, w1_raw)
+        wo_codes, wo_scales = weight("wo", wo_raw)
+        th = tile("th", [P, PACK, P], F32)
+        nc.scalar.activation(th[:], b_dealt, ACT.Tanh, bias=half_bias[:], scale=0.5)
+        th2 = tile("th2", [P, PACK, P], F32)
+        nc.scalar.activation(th2[:], th[:], ACT.Square)
+        h1 = tile("h1", [P, PACK, P], F32)
+        nc.scalar.activation(h1[:], a_dealt, ACT.Tanh)
+
+        dy_grouped = tile("dy_grouped", [P, PACK, P, PACK], BF16)
+        nc.vector.tensor_copy(
+            out=dy_grouped[:].rearrange("p t s i -> p s i t"),
+            in_=dy_raw[:].rearrange("p i (s t) -> p s i t", t=PACK),
+        )
+        dy_codes, dy_scales = quantize("dy", dy_grouped[:].rearrange("p t s i -> p (t s i)"), J)
+        c0_t = ps.tile([P, PACK, R], F32, name="c0_bank")
+        for t in range(PACK):
+            cols = slice(t * P, (t + 1) * P)
+            nc.tensor.matmul_mx(
+                out=c0_t[:, t, :], lhsT=dy_codes[:, cols].bitcast(FP8X4), lhsT_scale=dy_scales[:, cols],
+                rhs=wo_codes[:].bitcast(FP8X4), rhs_scale=wo_scales[:], start=True, stop=True,
+            )
+        upstream = tile("upstream", [P, PACK, R], F32)
+        for t in range(PACK):
+            nc.scalar.activation(upstream[:, t, :], c0_t[:, t, :], ACT.Copy, scale=js_cols[:, t : t + 1])
+
+        local = tile("local", [P, PACK, P], F32)
+        nc.vector.scalar_tensor_tensor(
+            out=local[:], in0=th2[:], scalar=1.0, in1=h1[:], op0=ALU.subtract, op1=ALU.mult
+        )
+        local_t = ps.tile([P, PACK, R], F32, name="local_bank")
+        for t in range(PACK):
+            nc.tensor.transpose(local_t[:, t, :], local[:, t, :], ident[:])
+
+        def turned_x(c):
+            picked = gather("x_picked%d" % c, x_win[c], slots2, BF16)
+            pairs = picked[:].bitcast(F32)
+            bank = ps2.tile([P, 2, P], F32, name="x_bank")
+            for u in range(2):
+                nc.tensor.transpose(bank[:, u, :], pairs[:, u : J // 2 : 2], ident[:])
+            grouped = tile("x_grouped%d" % c, [P, P * PACK], BF16)
+            nc.scalar.copy(
+                out=grouped[:].bitcast(F32).rearrange("p (k u) -> p k u", u=2),
+                in_=bank[:].rearrange("p u k -> p k u"),
+            )
+            return grouped
+
+        x_grouped = [turned_x(0)]
+
+        g_grouped = tile("g_grouped", [P, R, PACK], BF16)
+        nc.vector.scalar_tensor_tensor(
+            out=g_grouped[:], in0=local_t[:].rearrange("p t r -> p r t"), scalar=-0.25,
+            in1=upstream[:].rearrange("p t r -> p r t"), op0=ALU.mult, op1=ALU.mult,
+        )
+        g_codes, g_scales = quantize("g", g_grouped[:].rearrange("p r t -> p (r t)"), R)
+
+        out_rows = rows_by_four(out)
+        for name, blocks in (("early", range(0, PACK - 1)), ("last", range(PACK - 1, PACK))):
+            gw = ps.tile([P, len(blocks), R], F32, name=name + "_bank")
+            for n, c in enumerate(blocks):
+                if c + 1 < PACK:
+                    x_grouped.append(turned_x(c + 1))
+                x_codes, x_scales = quantize(
+                    "x%d" % c, x_grouped[c][:], P, "x_win%d" % (c + 1) if c + 1 < PACK else None
+                )
+                nc.tensor.matmul_mx(
+                    out=gw[:, n, :], lhsT=x_codes[:].bitcast(FP8X4), lhsT_scale=x_scales[:],
+                    rhs=g_codes[:].bitcast(FP8X4), rhs_scale=g_scales[:], start=True, stop=True,
+                )
+            span = slice(blocks.start, blocks.stop)
+            result = tile(name + "_result", [P, len(blocks), R], F32)
+            nc.vector.tensor_tensor(out=result[:], in0=gw[:], in1=old_sb[:, span, :], op=ALU.add)
+            nc.sync.dma_start(out=out_rows[:, span, :], in_=result[:])

@@ -105,8 +105,8 @@ def tile_attend_ctwotables_b_w_kernel(
             interleave(grouped[:], raw)
             return quantize(name, grouped[:].rearrange("p r i -> p (r i)"), R)
 
-        def layer(name, word_win, scale_win, slots, w_raw):
-            words = gather(name + "_words", word_win, slots, U16)
+        def layer(name, word_win, scale_win, slots, w_raw, words_tag):
+            words = gather(words_tag, word_win, slots, U16)
             scales = gather(name + "_scale_bytes", scale_win, slots, U8)
             w_codes, w_scales = weight(name + "_w", w_raw)
             acc = ps.tile([P, J], F32, name=name + "_bank")
@@ -116,8 +116,8 @@ def tile_attend_ctwotables_b_w_kernel(
             )
             return acc[:].rearrange("r (s t) -> r t s", t=PACK)
 
-        b_dealt = layer("b", word_win2, scale_win2, slots2, w2_raw)
-        a_dealt = layer("a", word_win1, scale_win1, slots1, w1_raw)
+        b_dealt = layer("b", word_win2, scale_win2, slots2, w2_raw, "b_words")
+        a_dealt = layer("a", word_win1, scale_win1, slots1, w1_raw, "b_w_grouped")
         wo_codes, wo_scales = weight("wo", wo_raw)
         th = tile("th", [P, PACK, P], F32)
         nc.scalar.activation(th[:], b_dealt, ACT.Tanh, bias=half_bias[:], scale=0.5)
@@ -143,7 +143,7 @@ def tile_attend_ctwotables_b_w_kernel(
         for t in range(PACK):
             nc.scalar.activation(upstream[:, t, :], c0_t[:, t, :], ACT.Copy, scale=js_cols[:, t : t + 1])
 
-        local = tile("local", [P, PACK, P], F32)
+        local = tile("dy_grouped", [P, PACK, P], F32)
         nc.vector.scalar_tensor_tensor(
             out=local[:], in0=th2[:], scalar=1.0, in1=h1[:], op0=ALU.subtract, op1=ALU.mult
         )
@@ -164,9 +164,9 @@ def tile_attend_ctwotables_b_w_kernel(
             )
             return grouped
 
-        x_grouped = [turned_x(0)]
+        x_grouped = [turned_x(0), turned_x(1)]
 
-        g_grouped = tile("g_grouped", [P, R, PACK], BF16)
+        g_grouped = tile("x_win1", [P, R, PACK], BF16)
         nc.vector.scalar_tensor_tensor(
             out=g_grouped[:], in0=local_t[:].rearrange("p t r -> p r t"), scalar=-0.25,
             in1=upstream[:].rearrange("p t r -> p r t"), op0=ALU.mult, op1=ALU.mult,
@@ -177,7 +177,7 @@ def tile_attend_ctwotables_b_w_kernel(
         for name, blocks in (("early", range(0, PACK - 1)), ("last", range(PACK - 1, PACK))):
             gw = ps.tile([P, len(blocks), R], F32, name=name + "_bank")
             for n, c in enumerate(blocks):
-                if c + 1 < PACK:
+                if 1 < c + 1 < PACK:
                     x_grouped.append(turned_x(c + 1))
                 x_codes, x_scales = quantize(
                     "x%d" % c, x_grouped[c][:], P, "x_win%d" % (c + 1) if c + 1 < PACK else None

@@ -143,7 +143,22 @@ def tile_attend_ctwotables_b_w_kernel(
         for t in range(PACK):
             nc.scalar.activation(upstream[:, t, :], c0_t[:, t, :], ACT.Copy, scale=js_cols[:, t : t + 1])
 
-        local = tile("dy_grouped", [P, PACK, P], F32)
+        def turn_x(c, grouped):
+            picked = gather("x_picked%d" % c, x_win[c], slots2, BF16)
+            pairs = picked[:].bitcast(F32)
+            bank = ps2.tile([P, 2, P], F32, name="x_bank")
+            for u in range(2):
+                nc.tensor.transpose(bank[:, u, :], pairs[:, u : J // 2 : 2], ident[:])
+            nc.scalar.copy(
+                out=grouped.bitcast(F32).rearrange("p (k u) -> p k u", u=2),
+                in_=bank[:].rearrange("p u k -> p k u"),
+            )
+
+        x_first = tile("x_first", [P, J], BF16)
+        x_middle = tile("x_middle", [P, 2 * J], BF16)
+        x_last = tile("x_last", [P, J], BF16)
+        turn_x(0, x_first[:])
+        local = tile("x_win0", [P, PACK, P], F32)
         nc.vector.scalar_tensor_tensor(
             out=local[:], in0=th2[:], scalar=1.0, in1=h1[:], op0=ALU.subtract, op1=ALU.mult
         )
@@ -151,42 +166,40 @@ def tile_attend_ctwotables_b_w_kernel(
         for t in range(PACK):
             nc.tensor.transpose(local_t[:, t, :], local[:, t, :], ident[:])
 
-        def turned_x(c):
-            picked = gather("x_picked%d" % c, x_win[c], slots2, BF16)
-            pairs = picked[:].bitcast(F32)
-            bank = ps2.tile([P, 2, P], F32, name="x_bank")
-            for u in range(2):
-                nc.tensor.transpose(bank[:, u, :], pairs[:, u : J // 2 : 2], ident[:])
-            grouped = tile("x_grouped%d" % c, [P, P * PACK], BF16)
-            nc.scalar.copy(
-                out=grouped[:].bitcast(F32).rearrange("p (k u) -> p k u", u=2),
-                in_=bank[:].rearrange("p u k -> p k u"),
-            )
-            return grouped
-
-        x_grouped = [turned_x(0), turned_x(1)]
-
-        g_grouped = tile("x_win1", [P, R, PACK], BF16)
+        turn_x(1, x_middle[:, :J])
+        first_q = quantize("x_first", x_first[:], P, "x_win1")
+        turn_x(2, x_middle[:, J:])
+        g_grouped = tile("x_win2", [P, R, PACK], BF16)
         nc.vector.scalar_tensor_tensor(
             out=g_grouped[:], in0=local_t[:].rearrange("p t r -> p r t"), scalar=-0.25,
             in1=upstream[:].rearrange("p t r -> p r t"), op0=ALU.mult, op1=ALU.mult,
         )
-        g_codes, g_scales = quantize("g", g_grouped[:].rearrange("p r t -> p (r t)"), R)
+        turn_x(3, x_last[:])
+        late_codes = tile("x_win3", [P, R + 2 * P], U32)
+        g_codes = late_codes[:, :R]
+        g_scales = tile("g_scales", [P, R], U8)
+        nc.vector.quantize_mx(
+            out=g_codes.bitcast(FP8X4), scales=g_scales[:], in_=g_grouped[:].rearrange("p r t -> p (r t)")
+        )
+        middle_scales = tile("middle_scales", [P, 2 * P], U8)
+        nc.vector.quantize_mx(out=late_codes[:, R:].bitcast(FP8X4), scales=middle_scales[:], in_=x_middle[:])
+        last_q = quantize("x_last", x_last[:], P)
+        x_q = [
+            (first_q[0][:], first_q[1][:]),
+            (late_codes[:, R : R + P], middle_scales[:, :P]),
+            (late_codes[:, R + P :], middle_scales[:, P:]),
+            (last_q[0][:], last_q[1][:]),
+        ]
 
         out_rows = rows_by_four(out)
         for name, blocks in (("early", range(0, PACK - 1)), ("last", range(PACK - 1, PACK))):
             gw = ps.tile([P, len(blocks), R], F32, name=name + "_bank")
             for n, c in enumerate(blocks):
-                if 1 < c + 1 < PACK:
-                    x_grouped.append(turned_x(c + 1))
-                x_codes, x_scales = quantize(
-                    "x%d" % c, x_grouped[c][:], P, "x_win%d" % (c + 1) if c + 1 < PACK else None
-                )
                 nc.tensor.matmul_mx(
-                    out=gw[:, n, :], lhsT=x_codes[:].bitcast(FP8X4), lhsT_scale=x_scales[:],
-                    rhs=g_codes[:].bitcast(FP8X4), rhs_scale=g_scales[:], start=True, stop=True,
+                    out=gw[:, n, :], lhsT=x_q[c][0].bitcast(FP8X4), lhsT_scale=x_q[c][1],
+                    rhs=g_codes.bitcast(FP8X4), rhs_scale=g_scales[:], start=True, stop=True,
                 )
             span = slice(blocks.start, blocks.stop)
-            result = tile(name + "_result", [P, len(blocks), R], F32)
+            result = tile("x_last" if name == "early" else "last_result", [P, len(blocks), R], F32)
             nc.vector.tensor_tensor(out=result[:], in0=gw[:], in1=old_sb[:, span, :], op=ALU.add)
             nc.sync.dma_start(out=out_rows[:, span, :], in_=result[:])

from contextlib import ExitStack

import concourse.mybir as mybir
from concourse.masks import make_identity

K, R, F, T, J = 512, 128, 512, 2048, 512
FLOPS = 2 * R * J * (K + K + F + K)

F32 = mybir.dt.float32
BF16 = mybir.dt.bfloat16
I32 = mybir.dt.int32
U32 = mybir.dt.uint32
U16 = mybir.dt.uint16
U8 = mybir.dt.uint8
FP8X4 = mybir.dt.float8_e4m3fn_x4
FP4X4 = mybir.dt.float4_e2m1fn_x4
ACT = mybir.ActivationFunctionType
ALU = mybir.AluOpType

P = 128
PACK = 4


def tile_attend_ctwotables_b_w_kernel(
    tc, tab_words, tab_scales, w1, tab2_words, tab2_scales, w2, bias, wo, dy, js, xrows, old, offs, offs2, out
):
    nc = tc.nc
    with ExitStack() as ctx:
        sb = ctx.enter_context(tc.tile_pool(name="sb", bufs=1))
        ps = ctx.enter_context(tc.psum_pool(name="ps", bufs=1))
        ps2 = ctx.enter_context(tc.psum_pool(name="ps2", bufs=2))

        def tile(name, shape, dtype):
            return sb.tile(shape, dtype, name=name, align_bytes=64)

        def rows_by_four(src):
            return src.rearrange("(p i) c -> p i c", i=PACK)

        def load_words(name, words, lst):
            word_win = tile(name + "_word_win", [P, T], U16)
            nc.sync.dma_start(out=word_win[:].bitcast(I32), in_=words[0].bitcast(I32))
            offsets = tile(name + "_offsets", [P, J // 16], U16)
            nc.sync.dma_start(offsets[:], lst)
            return word_win, offsets

        def load_scales(name, scales):
            scale_win = tile(name + "_scale_win", [P, T], U8)
            nc.vector.memset(scale_win[:].bitcast(I32), 0)
            for q in range(4):
                nc.sync.dma_start(
                    out=scale_win[32 * q : 32 * q + 4, :].bitcast(I32),
                    in_=scales[0, 4 * q : 4 * q + 4, :].bitcast(I32),
                )
            return scale_win

        def load(name, src, shape):
            raw = tile(name, shape, F32)
            nc.sync.dma_start(out=raw[:], in_=src)
            return raw

        bias_col = tile("bias_col", [P, 1], F32)
        nc.gpsimd.dma_start(out=bias_col[:], in_=bias)
        js_cols = tile("js_cols", [P, PACK], F32)
        nc.gpsimd.dma_start(out=js_cols[:], in_=js.rearrange("o (p t) -> (o p) t", t=PACK))
        ident = tile("ident", [P, P], F32)
        make_identity(nc, ident[:])

        word_win2, slots2 = load_words("t2", tab2_words, offs2)
        scale_win2 = load_scales("t2", tab2_scales)
        w2_raw = load("w2_raw", rows_by_four(w2), [P, PACK, R])
        word_win1, slots1 = load_words("t1", tab_words, offs)
        w1_raw = load("w1_raw", rows_by_four(w1), [P, PACK, R])
        scale_win1 = load_scales("t1", tab_scales)
        wo_raw = load("wo_raw", rows_by_four(wo), [P, PACK, R])
        dy_raw = load("dy_raw", rows_by_four(dy), [P, PACK, J])
        x_rows = rows_by_four(xrows)
        x_win = [load("x_win%d" % c, x_rows[:, c, :], [P, T]) for c in range(PACK)]
        old_sb = load("old_sb", rows_by_four(old), [P, PACK, R])

        half_bias = tile("half_bias", [P, 1], F32)
        nc.gpsimd.tensor_scalar(
            out=half_bias[:], in0=bias_col[:], scalar1=0.5, scalar2=0.0, op0=ALU.mult, op1=ALU.add
        )

        def quantize(name, grouped, width, codes_tag=None):
            codes = tile(codes_tag or name + "_codes", [P, width], U32)
            scales = tile(name + "_scales", [P, width], U8)
            nc.vector.quantize_mx(out=codes[:].bitcast(FP8X4), scales=scales[:], in_=grouped)
            return codes, scales

        def interleave(dst, raw):
            nc.scalar.activation(
                dst.rearrange("p (c n) i -> p c i n", n=4),
                raw[:].rearrange("p i (c n) -> p c i n", n=4),
                ACT.Copy,
            )

        def gather(name, window, offsets, dtype):
            picked = tile(name, [P, J], dtype)
            nc.vector.tensor_copy(picked[:], window[:].indirect(offsets[:]))
            return picked

        def weight(name, raw):
            grouped = tile(name + "_grouped", [P, R, PACK], BF16)
            interleave(grouped[:], raw)
            return quantize(name, grouped[:].rearrange("p r i -> p (r i)"), R)

        def layer(name, word_win, scale_win, slots, w_raw, words_tag):
            words = gather(words_tag, word_win, slots, U16)
            scales = gather(name + "_scale_bytes", scale_win, slots, U8)
            w_codes, w_scales = weight(name + "_w", w_raw)
            acc = ps.tile([P, J], F32, name=name + "_bank")
            nc.tensor.matmul_mx(
                out=acc[:], lhsT=w_codes[:].bitcast(FP8X4), lhsT_scale=w_scales[:],
                rhs=words[:].bitcast(FP4X4), rhs_scale=scales[:], start=True, stop=True,
            )
            return acc[:].rearrange("r (s t) -> r t s", t=PACK)

        b_dealt = layer("b", word_win2, scale_win2, slots2, w2_raw, "b_words")
        a_dealt = layer("a", word_win1, scale_win1, slots1, w1_raw, "b_w_grouped")
        wo_codes, wo_scales = weight("wo", wo_raw)
        th = tile("th", [P, PACK, P], F32)
        nc.scalar.activation(th[:], b_dealt, ACT.Tanh, bias=half_bias[:], scale=0.5)
        th2 = tile("th2", [P, PACK, P], F32)
        nc.scalar.activation(th2[:], th[:], ACT.Square)
        h1 = tile("h1", [P, PACK, P], F32)
        nc.scalar.activation(h1[:], a_dealt, ACT.Tanh)

        dy_grouped = tile("dy_grouped", [P, PACK, P, PACK], BF16)
        nc.vector.tensor_copy(
            out=dy_grouped[:].rearrange("p t s i -> p s i t"),
            in_=dy_raw[:].rearrange("p i (s t) -> p s i t", t=PACK),
        )
        dy_codes, dy_scales = quantize("dy", dy_grouped[:].rearrange("p t s i -> p (t s i)"), J)
        c0_t = ps.tile([P, PACK, R], F32, name="c0_bank")
        for t in range(PACK):
            cols = slice(t * P, (t + 1) * P)
            nc.tensor.matmul_mx(
                out=c0_t[:, t, :], lhsT=dy_codes[:, cols].bitcast(FP8X4), lhsT_scale=dy_scales[:, cols],
                rhs=wo_codes[:].bitcast(FP8X4), rhs_scale=wo_scales[:], start=True, stop=True,
            )
        upstream = tile("upstream", [P, PACK, R], F32)
        for t in range(PACK):
            nc.scalar.activation(upstream[:, t, :], c0_t[:, t, :], ACT.Copy, scale=js_cols[:, t : t + 1])

        def turn_x(c, grouped):
            picked = gather("x_picked%d" % c, x_win[c], slots2, BF16)
            pairs = picked[:].bitcast(F32)
            bank = ps2.tile([P, 2, P], F32, name="x_bank")
            for u in range(2):
                nc.tensor.transpose(bank[:, u, :], pairs[:, u : J // 2 : 2], ident[:])
            nc.scalar.copy(
                out=grouped.bitcast(F32).rearrange("p (k u) -> p k u", u=2),
                in_=bank[:].rearrange("p u k -> p k u"),
            )

        x_first = tile("x_first", [P, J], BF16)
        x_middle = tile("x_middle", [P, 2 * J], BF16)
        x_last = tile("x_last", [P, J], BF16)
        turn_x(0, x_first[:])
        local = tile("x_win0", [P, PACK, P], F32)
        nc.vector.scalar_tensor_tensor(
            out=local[:], in0=th2[:], scalar=1.0, in1=h1[:], op0=ALU.subtract, op1=ALU.mult
        )
        local_t = ps.tile([P, PACK, R], F32, name="local_bank")
        for t in range(PACK):
            nc.tensor.transpose(local_t[:, t, :], local[:, t, :], ident[:])

        turn_x(1, x_middle[:, :J])
        first_q = quantize("x_first", x_first[:], P, "x_win1")
        turn_x(2, x_middle[:, J:])
        g_grouped = tile("x_win2", [P, R, PACK], BF16)
        nc.vector.scalar_tensor_tensor(
            out=g_grouped[:], in0=local_t[:].rearrange("p t r -> p r t"), scalar=-0.25,
            in1=upstream[:].rearrange("p t r -> p r t"), op0=ALU.mult, op1=ALU.mult,
        )
        turn_x(3, x_last[:])
        late_codes = tile("x_win3", [P, R + 2 * P], U32)
        g_codes = late_codes[:, :R]
        g_scales = tile("g_scales", [P, R], U8)
        nc.vector.quantize_mx(
            out=g_codes.bitcast(FP8X4), scales=g_scales[:], in_=g_grouped[:].rearrange("p r t -> p (r t)")
        )
        middle_scales = tile("middle_scales", [P, 2 * P], U8)
        nc.vector.quantize_mx(out=late_codes[:, R:].bitcast(FP8X4), scales=middle_scales[:], in_=x_middle[:])
        last_q = quantize("x_last", x_last[:], P)
        x_q = [
            (first_q[0][:], first_q[1][:]),
            (late_codes[:, R : R + P], middle_scales[:, :P]),
            (late_codes[:, R + P :], middle_scales[:, P:]),
            (last_q[0][:], last_q[1][:]),
        ]

        out_rows = rows_by_four(out)
        for name, blocks in (("early", range(0, PACK - 1)), ("last", range(PACK - 1, PACK))):
            gw = ps.tile([P, len(blocks), R], F32, name=name + "_bank")
            for n, c in enumerate(blocks):
                nc.tensor.matmul_mx(
                    out=gw[:, n, :], lhsT=x_q[c][0].bitcast(FP8X4), lhsT_scale=x_q[c][1],
                    rhs=g_codes.bitcast(FP8X4), rhs_scale=g_scales[:], start=True, stop=True,
                )
            span = slice(blocks.start, blocks.stop)
            result = tile("x_last" if name == "early" else "last_result", [P, len(blocks), R], F32)
            nc.vector.tensor_tensor(out=result[:], in0=gw[:], in1=old_sb[:, span, :], op=ALU.add)
            nc.sync.dma_start(out=out_rows[:, span, :], in_=result[:])
